import numpy as np
import ml_dtypes


def mxq(x, axis, fmt="e4m3"):
    dtype, down = {"e4m3": (ml_dtypes.float8_e4m3fn, 7), "e5m2": (ml_dtypes.float8_e5m2, 14)}[fmt]
    v = np.moveaxis(np.asarray(x, np.float32).astype(ml_dtypes.bfloat16).astype(np.float64), axis, -1)
    blocks = v.reshape(v.shape[:-1] + (-1, 32))
    amax = np.abs(blocks).max(-1, keepdims=True)
    byte = np.maximum(np.where(amax > 0, np.frexp(amax)[1] - 1 + 127, 0) - down, 1)
    scale = np.exp2(byte - 127.0)
    codes = (blocks / scale).astype(np.float32).astype(dtype).astype(np.float64)
    return np.moveaxis((codes * scale).reshape(v.shape), -1, axis)


WIDE = False


def mx_kscale(k):
    if not WIDE:
        return np.ones(k)
    levels = np.array([10, -10, 5, -5, 0])
    if k % 512:
        return np.exp2(np.random.permutation(np.resize(levels, k // 32))).repeat(32)
    a = np.empty((k // 512, 16))
    for p in range(k // 512):
        a[p, :8] = np.random.permutation(np.resize(levels, 8))
        for g in range(8):
            far = levels[np.abs(levels - a[p, g]) >= 10]
            a[p, g + 8] = far[np.random.randint(len(far))]
    return np.exp2(a.ravel()).repeat(32)


def f64(x):
    return np.asarray(x).astype(np.float64)


def striped(idx):
    return np.tile(np.asarray(idx).reshape(-1, 16).T, (8, 1)).astype(np.uint16)


def unstriped(offs):
    return offs[:16].T.reshape(-1).astype(np.int64)


E2M1 = np.array([0.0, 0.5, 1.0, 1.5, 2.0, 3.0, 4.0, 6.0, -0.0, -0.5, -1.0, -1.5, -2.0, -3.0, -4.0, -6.0])


def pack_weight(w, fmt):
    k, n = w.shape
    w = f64(np.asarray(w, np.float32).astype(ml_dtypes.bfloat16)).reshape(k // 32, 32, n)
    amax = np.abs(w).max(1)
    if fmt == "e4m3":
        byte = np.frexp(amax)[1] - 1 + 127 - 7
    else:
        mant, ex = np.frexp(amax / 6.0)
        byte = np.where(mant > 0.5, ex, ex - 1) + 127
    byte = np.clip(np.where(amax > 0, byte, 1), 1, 254)
    scaled = (w * np.exp2(127.0 - byte)[:, None, :]).reshape(k, n).astype(np.float32)
    by_word = np.ascontiguousarray(scaled.reshape(k // 512, 128, 4, n).transpose(0, 1, 3, 2))
    if fmt == "e4m3":
        words = by_word.astype(ml_dtypes.float8_e4m3fn).view(np.uint8)
    else:
        c = by_word.astype(ml_dtypes.float4_e2m1fn).view(np.uint8) & 0xF
        words = (c[..., 0::2] | (c[..., 1::2] << 4)).reshape(k // 512, 128, 2 * n)
    return np.ascontiguousarray(words), np.ascontiguousarray(byte.astype(np.uint8).reshape(k // 512, 16, n))


def unpack_weight(words, scales, fmt):
    g, _, n = scales.shape
    words = np.ascontiguousarray(words).reshape(g, 128, n, -1)
    if fmt == "e4m3":
        vals = words.view(ml_dtypes.float8_e4m3fn).astype(np.float64)
    else:
        nib = np.empty((g, 128, n, 4), np.uint8)
        nib[..., 0::2] = words & 0xF
        nib[..., 1::2] = words >> 4
        vals = E2M1[nib]
    vals = vals * np.repeat(np.exp2(scales.astype(np.float64) - 127.0), 8, axis=1)[..., None]
    return vals.transpose(0, 1, 3, 2).reshape(g * 512, n)


def sigmoid(v):
    return 1.0 / (1.0 + np.exp(-v))


D, E, T, I, Q, G, B = 512, 512, 2048, 512, 128, 64, 8


def setup_inputs():
    n = np.random.standard_normal
    idx = np.random.permutation(T)[:I]
    fd = mx_kscale(D)
    fi = mx_kscale(I)
    ti = np.ones(T)
    ti[idx] = fi
    keysp = pack_weight(n((D, T)) / fd[:, None], "e2m1")
    return {
        "query": (n((D, Q)) * 0.8 / np.sqrt(D) * fd[:, None]).astype(np.float32),
        "keys_words": keysp[0],
        "keys_scales": keysp[1],
        "steep": (np.random.uniform(2.0, 8.0, (Q, 1))).astype(np.float32),
        "dquery": (n((D, Q)) * 0.6 / np.sqrt(D) * fd[:, None]).astype(np.float32),
        "os": (np.random.uniform(4.0, 16.0, (1, I)) * fi).astype(np.float32),
        "vals": (n((E, T)) / ti).astype(np.float32),
        "offs": striped(idx),
    }


def reference(query, keys_words, keys_scales, steep, dquery, os, vals, offs):
    idx = unstriped(offs)
    keysu = unpack_weight(keys_words, keys_scales, "e2m1")
    queryq = mxq(f64(query), 0, "e4m3")
    keysidxg = keysu[:, idx]
    a = queryq.T @ keysidxg
    dqueryq = mxq(f64(dquery), 0, "e4m3")
    ta = dqueryq.T @ keysidxg
    m1 = a.reshape(Q, G, I // G).mean(axis=2)
    m2 = m1.reshape(Q, B, G // B).mean(axis=2)
    mr = np.repeat(m2, G // B, axis=1)
    g1 = sigmoid((m1 - mr) * f64(steep))
    gr = np.repeat(g1, I // G, axis=1)
    p = np.exp(a) * gr
    z = np.sum(p, axis=1, keepdims=True)
    tm1 = ta.reshape(Q, G, I // G).mean(axis=2)
    tm2 = tm1.reshape(Q, B, G // B).mean(axis=2)
    tmr = np.repeat(tm2, G // B, axis=1)
    tg1 = (tm1 - tmr) * f64(steep) * g1 * (1.0 - g1)
    tgr = np.repeat(tg1, I // G, axis=1)
    tp = ta * np.exp(a) * gr + tgr * np.exp(a)
    tz = np.sum(tp, axis=1, keepdims=True)
    tw = (tp - tz * p / z) / z
    wo1 = tw * f64(os)
    wt1 = wo1.T
    vt1 = f64(vals)[:, idx].T
    wt1q = mxq(wt1, 0, "e4m3")
    vt1q = mxq(vt1, 0, "e4m3")
    o = wt1q.T @ vt1q
    return o

@@ -1,0 +1,199 @@
+import math
+from contextlib import ExitStack
+
+import concourse.mybir as mybir
+from concourse.masks import make_identity
+
+D, E, T, I, Q, G, B = 512, 512, 2048, 512, 128, 64, 8
+FLOPS = 2 * 2 * D * Q * I + 2 * I * Q * E
+
+F32 = mybir.dt.float32
+BF16 = mybir.dt.bfloat16
+I32 = mybir.dt.int32
+U32 = mybir.dt.uint32
+U16 = mybir.dt.uint16
+U8 = mybir.dt.uint8
+FP8X4 = mybir.dt.float8_e4m3fn_x4
+FP4X4 = mybir.dt.float4_e2m1fn_x4
+ALU = mybir.AluOpType
+ACT = mybir.ActivationFunctionType
+AX = mybir.AxisListType
+
+P = 128
+PACK = 4
+GROUP = I // G
+SOFT = 8.0
+
+
+def tile_attend_ttblockcontrast_kernel(tc, query, keys_words, keys_scales, steep, dquery, slot_factor, vals, offs, out):
+    nc = tc.nc
+    blocks = E // P
+    with ExitStack() as ctx:
+        sb = ctx.enter_context(tc.tile_pool(name="sb", bufs=1))
+        ps = ctx.enter_context(tc.psum_pool(name="ps", bufs=1))
+
+        offsets = sb.tile([P, I // 16], U16, name="offsets")
+        nc.sync.dma_start(offsets[:], offs)
+
+        key_bytes = sb.tile([P, T], U8, name="key_bytes", tag="key_bytes", align_bytes=64)
+        nc.vector.memset(key_bytes[:].bitcast(I32), 0)
+        for quad in range(4):
+            nc.scalar.dma_start(
+                out=key_bytes[32 * quad : 32 * quad + 4, :].bitcast(I32),
+                in_=keys_scales[0, 4 * quad : 4 * quad + 4, :].bitcast(I32),
+            )
+        warm_in = sb.tile([P, 1], F32, name="warm_in")
+        warm_out = sb.tile([P, 1], F32, name="warm_out")
+        nc.vector.memset(warm_in[:], 0.0)
+        nc.scalar.activation(warm_out[:], warm_in[:], ACT.Exp)
+
+        key_words = sb.tile([P, T], U16, name="key_words", align_bytes=64)
+        nc.sync.dma_start(out=key_words[:].bitcast(I32), in_=keys_words[0].bitcast(I32))
+        q_raw = sb.tile([P, PACK, Q], F32, name="q_raw", tag="pool2", align_bytes=64)
+        nc.sync.dma_start(out=q_raw[:], in_=query.rearrange("(p j) w -> p j w", j=PACK))
+        dq_raw = sb.tile([P, PACK, Q], F32, name="dq_raw", tag="pool3", align_bytes=64)
+        nc.sync.dma_start(out=dq_raw[:], in_=dquery.rearrange("(p j) w -> p j w", j=PACK))
+        steep_col = sb.tile([P, 1], F32, name="steep_col")
+        nc.gpsimd.dma_start(out=steep_col[:], in_=steep)
+        factor_cols = sb.tile([P, PACK], F32, name="factor_cols")
+        nc.gpsimd.dma_start(out=factor_cols[:], in_=slot_factor.rearrange("o (p t) -> p (o t)", t=PACK))
+        ident = sb.tile([P, P], F32, name="ident")
+        make_identity(nc, ident[:])
+        half_slope = sb.tile([P, 1], F32, name="half_slope")
+        nc.gpsimd.tensor_scalar(half_slope[:], steep_col[:], 0.5 / GROUP, 0.0, ALU.mult, ALU.add)
+        neg_half_slope = sb.tile([P, 1], F32, name="neg_half_slope")
+        nc.gpsimd.tensor_scalar(neg_half_slope[:], steep_col[:], -0.5 / GROUP, 0.0, ALU.mult, ALU.add)
+
+        k_codes = sb.tile([P, I], U16, name="k_codes", align_bytes=64)
+        nc.vector.tensor_copy(k_codes[:], key_words[:].indirect(offsets[:]))
+
+        k_scales = sb.tile([P, I], U8, name="k_scales", align_bytes=64)
+        nc.vector.tensor_copy(k_scales[:], key_bytes[:].indirect(offsets[:]))
+
+        q_codes = []
+        q_scales = []
+        for name, raw in (("q", q_raw), ("dq", dq_raw)):
+            grouped = sb.tile([P, Q, PACK], BF16, name=name + "_grouped", align_bytes=64)
+            nc.scalar.copy(
+                out=grouped[:].rearrange("p (c i) t -> p c t i", i=4),
+                in_=raw[:].rearrange("p t (c i) -> p c t i", i=4),
+            )
+            codes = sb.tile([P, Q], U32, name=name + "_codes", align_bytes=64)
+            scales = sb.tile([P, Q], U8, name=name + "_scales", align_bytes=64)
+            nc.vector.quantize_mx(out=codes[:].bitcast(FP8X4), scales=scales[:], in_=grouped[:].rearrange("p w j -> p (w j)"))
+            q_codes.append(codes)
+            q_scales.append(scales)
+
+        pool = []
+        for j in range(blocks):
+            rows = sb.tile([P, T], F32, name="pool%d" % j, tag="pool%d" % j, align_bytes=64)
+            nc.sync.dma_start(out=rows[:], in_=vals[j * P : (j + 1) * P, :])
+            pool.append(rows)
+
+        a_ps = ps.tile([P, I], F32, name="a_ps", tag="a_ps")
+        ta_ps = ps.tile([P, I], F32, name="ta_ps")
+        for acc, codes, scales in ((a_ps, q_codes[0], q_scales[0]), (ta_ps, q_codes[1], q_scales[1])):
+            nc.tensor.matmul_mx(
+                out=acc[:], lhsT=codes[:].bitcast(FP8X4), lhsT_scale=scales[:],
+                rhs=k_codes[:].bitcast(FP4X4), rhs_scale=k_scales[:], start=True, stop=True,
+            )
+
+        soft = sb.tile([P, I], BF16, name="soft")
+        soft_sum = sb.tile([P, 1], F32, name="soft_sum")
+        nc.scalar.activation(soft[:], a_ps[:], ACT.Exp, scale=1.0 / SOFT, accum_out=soft_sum[:])
+        neg_shift = sb.tile([P, 1], F32, name="neg_shift")
+        nc.scalar.activation(
+            neg_shift[:], soft_sum[:].bitcast(U32), ACT.Copy, scale=-SOFT * math.log(2.0) / 2.0**23,
+            bias=SOFT * (127.0 * math.log(2.0) + math.log(I)),
+        )
+        e = sb.tile([P, I], F32, name="e")
+        nc.scalar.activation(e[:], a_ps[:], ACT.Exp, bias=neg_shift[:])
+
+        sums = sb.tile([P, 2 * G], F32, name="sums", tag="pool0", align_bytes=64)
+        nc.vector.tensor_reduce(sums[:, 0:G], a_ps[:].rearrange("p (g r) -> p g r", r=GROUP), AX.X, ALU.add)
+        nc.vector.tensor_reduce(sums[:, G : 2 * G], ta_ps[:].rearrange("p (g r) -> p g r", r=GROUP), AX.X, ALU.add)
+        block_sums = sb.tile([P, 2 * B], F32, name="block_sums")
+        per_block = G // B
+        nc.vector.tensor_reduce(block_sums[:], sums[:].rearrange("p (b g) -> p b g", g=per_block), AX.X, ALU.add)
+        diff = sb.tile([P, 2 * G], F32, name="diff")
+        nc.vector.scalar_tensor_tensor(
+            diff[:].rearrange("p (b g) -> p b g", g=per_block),
+            block_sums[:].unsqueeze(2).to_broadcast([P, 2 * B, per_block]), -1.0 / per_block,
+            sums[:].rearrange("p (b g) -> p b g", g=per_block), ALU.mult, ALU.add,
+        )
+        th = sb.tile([P, G], F32, name="th")
+        nc.scalar.activation(th[:], diff[:, 0:G], ACT.Tanh, scale=half_slope[:])
+
+        factor_ps = ps.tile([P, PACK, P], F32, name="factor_ps", tag="a_ps")
+        for t in range(PACK):
+            nc.tensor.transpose(factor_ps[:, t, :], factor_cols[:, t : t + 1].to_broadcast([P, P]), ident[:])
+
+        def by_group(tile):
+            return tile[:].rearrange("p (g r) -> p g r", r=GROUP)
+
+        def spread(tile):
+            return tile[:].unsqueeze(2).to_broadcast([P, G, GROUP])
+
+        p = sb.tile([P, I], F32, name="p")
+        z = sb.tile([P, 1], F32, name="z")
+        nc.vector.scalar_tensor_tensor(by_group(p), spread(th), 1.0, by_group(e), ALU.add, ALU.mult, accum_out=z[:])
+        h = sb.tile([P, G], F32, name="h")
+        nc.vector.scalar_tensor_tensor(h[:], th[:], 1.0, diff[:, G : 2 * G], ALU.subtract, ALU.mult)
+        rz = sb.tile([P, 1], F32, name="rz")
+        nc.vector.reciprocal(rz[:], z[:])
+        u = sb.tile([P, I], F32, name="u")
+        nc.vector.scalar_tensor_tensor(by_group(u), spread(h), neg_half_slope[:], by_group(ta_ps), ALU.mult, ALU.add)
+        tp = sb.tile([P, I], F32, name="tp", tag="pool2", align_bytes=64)
+        c = sb.tile([P, 1], F32, name="c")
+        nc.vector.scalar_tensor_tensor(tp[:], u[:], rz[:], p[:], ALU.mult, ALU.mult, accum_out=c[:])
+        v = sb.tile([P, I], F32, name="v")
+        nc.vector.scalar_tensor_tensor(v[:], u[:], c[:], p[:], ALU.subtract, ALU.mult)
+        w = sb.tile([P, I], BF16, name="w")
+        nc.vector.scalar_tensor_tensor(
+            w[:].rearrange("p (n t) -> p n t", t=PACK), v[:].rearrange("p (n t) -> p n t", t=PACK), rz[:],
+            factor_ps[:].rearrange("p t n -> p n t"), ALU.mult, ALU.mult,
+        )
+
+        def turn_and_quantize(name, rows, bank, codes, grouped_tag):
+            words = rows[:].bitcast(F32)
+            for half in range(2):
+                nc.tensor.transpose(bank[:, half, :], words[:, half : I // 2 : 2], ident[:])
+            grouped = sb.tile([P, P * PACK], BF16, name=name + "_grouped", tag=grouped_tag, align_bytes=64)
+            nc.scalar.copy(
+                out=grouped[:].bitcast(F32).rearrange("p (x u) -> p x u", u=2), in_=bank[:].rearrange("p u x -> p x u")
+            )
+            scales = sb.tile([P, P], U8, name=name + "_scales", align_bytes=64)
+            nc.vector.quantize_mx(out=codes.bitcast(FP8X4), scales=scales[:], in_=grouped[:])
+            return scales
+
+        v_banks = [ps.tile([P, 2, P], F32, name="v_bank%d" % n) for n in range(2)]
+        listed = [sb.tile([P, I], BF16, name="listed%d" % j) for j in range(blocks)]
+        rounded = sb.tile([P, T], BF16, name="rounded", tag="rounded", align_bytes=64)
+        for j in range(blocks):
+            if j == 1:
+                for c0 in range(0, T, 512):
+                    nc.scalar.activation(rounded[:, c0 : c0 + 512], pool[j][:, c0 : c0 + 512], ACT.Copy)
+                nc.scalar.activation(listed[j][:], rounded[:].indirect(offsets[:]), ACT.Copy)
+            else:
+                nc.vector.tensor_copy(listed[j][:], pool[j][:].indirect(offsets[:]))
+        late_codes = sb.tile([P, 3, P], U32, name="late_codes", tag="pool3", align_bytes=64)
+        own_codes = sb.tile([P, 2, P], U32, name="own_codes", align_bytes=64)
+        w_bank = ps.tile([P, 2, P], F32, name="w_bank")
+        w_codes = late_codes[:, 0, :]
+        w_scales = turn_and_quantize("w", w, w_bank, w_codes, "rounded")
+        v_codes = [own_codes[:, 0, :], late_codes[:, 1, :], late_codes[:, 2, :], own_codes[:, 1, :]]
+        head_ps = ps.tile([P, (blocks - 1) * P], F32, name="head_ps")
+        tail_ps = ps.tile([P, P], F32, name="tail_ps")
+        for j in range(blocks):
+            scales = turn_and_quantize("v%d" % j, listed[j], v_banks[j % 2], v_codes[j], "v%d_grouped" % j)
+            acc = head_ps[:, j * P : (j + 1) * P] if j < blocks - 1 else tail_ps[:]
+            nc.tensor.matmul_mx(
+                out=acc, lhsT=w_codes.bitcast(FP8X4), lhsT_scale=w_scales[:],
+                rhs=v_codes[j].bitcast(FP8X4), rhs_scale=scales[:], start=True, stop=True,
+            )
+        head = sb.tile([P, (blocks - 1) * P], F32, name="head")
+        nc.scalar.copy(out=head[:], in_=head_ps[:])
+        nc.sync.dma_start(out=out[:, 0 : (blocks - 1) * P], in_=head[:])
+        tail = sb.tile([P, P], F32, name="tail")
+        nc.scalar.copy(out=tail[:], in_=tail_ps[:])
+        nc.sync.dma_start(out=out[:, (blocks - 1) * P : E], in_=tail[:])

@@ -22,178 +22,214 @@ AX = mybir.AxisListType
 P = 128
 PACK = 4
 GROUP = I // G
+PER_BLOCK = G // B
+HALF = I // 2
+HALF_G = G // 2
 SOFT = 8.0
+CHUNK = 512
 
 
 def tile_attend_ttblockcontrast_kernel(tc, query, keys_words, keys_scales, steep, dquery, slot_factor, vals, offs, out):
     nc = tc.nc
-    blocks = E // P
     with ExitStack() as ctx:
         sb = ctx.enter_context(tc.tile_pool(name="sb", bufs=1))
         ps = ctx.enter_context(tc.psum_pool(name="ps", bufs=1))
 
+        def tile(name, shape, dtype, tag=None):
+            return sb.tile(shape, dtype, name=name, tag=tag or name, align_bytes=64)
+
+        def bank(name, shape, tag=None):
+            return ps.tile(shape, F32, name=name, tag=tag or name)
+
+        def by_group(ap):
+            return ap.rearrange("p (g r) -> p g r", r=GROUP)
+
+        def spread(ap):
+            return ap.unsqueeze(2).to_broadcast([P, ap.shape[1], GROUP])
+
         offsets = sb.tile([P, I // 16], U16, name="offsets")
         nc.sync.dma_start(offsets[:], offs)
+        half_lists = [offsets[:, 0 : HALF // 16], offsets[:, HALF // 16 : I // 16]]
 
-        key_bytes = sb.tile([P, T], U8, name="key_bytes", tag="key_bytes", align_bytes=64)
-        nc.vector.memset(key_bytes[:].bitcast(I32), 0)
+        key_words = tile("key_words", [P, T], U16)
+        nc.sync.dma_start(out=key_words[:].bitcast(I32), in_=keys_words[0].bitcast(I32))
+        key_bytes = tile("key_bytes", [P, T], U8)
+        nc.gpsimd.memset(key_bytes[:].bitcast(I32), 0)
         for quad in range(4):
-            nc.scalar.dma_start(
+            nc.sync.dma_start(
                 out=key_bytes[32 * quad : 32 * quad + 4, :].bitcast(I32),
                 in_=keys_scales[0, 4 * quad : 4 * quad + 4, :].bitcast(I32),
             )
-        warm_in = sb.tile([P, 1], F32, name="warm_in")
-        warm_out = sb.tile([P, 1], F32, name="warm_out")
+        q_raw = tile("q_raw", [P, PACK, Q], F32)
+        nc.sync.dma_start(out=q_raw[:], in_=query.rearrange("(p j) w -> p j w", j=PACK))
+        dq_raw = tile("dq_raw", [P, PACK, Q], F32)
+        nc.sync.dma_start(out=dq_raw[:], in_=dquery.rearrange("(p j) w -> p j w", j=PACK))
+        pool = [tile("pool%d" % j, [P, T], F32) for j in range(4)]
+        nc.sync.dma_start(out=pool[0][:], in_=vals[0:P, :])
+        steep_col = tile("steep_col", [P, 1], F32)
+        nc.sync.dma_start(out=steep_col[:], in_=steep)
+        factor_cols = tile("factor_cols", [P, PACK], F32)
+        nc.sync.dma_start(out=factor_cols[:], in_=slot_factor.rearrange("o (p t) -> p (o t)", t=PACK))
+        for j in range(1, 4):
+            nc.sync.dma_start(out=pool[j][:], in_=vals[j * P : (j + 1) * P, :])
+
+        warm_in = tile("warm_in", [P, 1], F32)
+        warm_out = tile("warm_out", [P, 1], F32)
         nc.vector.memset(warm_in[:], 0.0)
         nc.scalar.activation(warm_out[:], warm_in[:], ACT.Exp)
 
-        key_words = sb.tile([P, T], U16, name="key_words", align_bytes=64)
-        nc.sync.dma_start(out=key_words[:].bitcast(I32), in_=keys_words[0].bitcast(I32))
-        q_raw = sb.tile([P, PACK, Q], F32, name="q_raw", tag="pool2", align_bytes=64)
-        nc.sync.dma_start(out=q_raw[:], in_=query.rearrange("(p j) w -> p j w", j=PACK))
-        dq_raw = sb.tile([P, PACK, Q], F32, name="dq_raw", tag="pool3", align_bytes=64)
-        nc.sync.dma_start(out=dq_raw[:], in_=dquery.rearrange("(p j) w -> p j w", j=PACK))
-        steep_col = sb.tile([P, 1], F32, name="steep_col")
-        nc.gpsimd.dma_start(out=steep_col[:], in_=steep)
-        factor_cols = sb.tile([P, PACK], F32, name="factor_cols")
-        nc.gpsimd.dma_start(out=factor_cols[:], in_=slot_factor.rearrange("o (p t) -> p (o t)", t=PACK))
-        ident = sb.tile([P, P], F32, name="ident")
+        ident = tile("ident", [P, P], F32)
         make_identity(nc, ident[:])
-        half_slope = sb.tile([P, 1], F32, name="half_slope")
+        half_slope = tile("half_slope", [P, 1], F32)
         nc.gpsimd.tensor_scalar(half_slope[:], steep_col[:], 0.5 / GROUP, 0.0, ALU.mult, ALU.add)
-        neg_half_slope = sb.tile([P, 1], F32, name="neg_half_slope")
+        neg_half_slope = tile("neg_half_slope", [P, 1], F32)
         nc.gpsimd.tensor_scalar(neg_half_slope[:], steep_col[:], -0.5 / GROUP, 0.0, ALU.mult, ALU.add)
 
-        k_codes = sb.tile([P, I], U16, name="k_codes", align_bytes=64)
-        nc.vector.tensor_copy(k_codes[:], key_words[:].indirect(offsets[:]))
+        def gather_keys(half, codes_tag, scales_tag):
+            codes = tile("k_codes%d" % half, [P, HALF], U16, codes_tag)
+            nc.vector.tensor_copy(codes[:], key_words[:].indirect(half_lists[half]))
+            scales = tile("k_scales%d" % half, [P, HALF], U8, scales_tag)
+            nc.vector.tensor_copy(scales[:], key_bytes[:].indirect(half_lists[half]))
+            return codes, scales
 
-        k_scales = sb.tile([P, I], U8, name="k_scales", align_bytes=64)
-        nc.vector.tensor_copy(k_scales[:], key_bytes[:].indirect(offsets[:]))
-
-        q_codes = []
-        q_scales = []
-        for name, raw in (("q", q_raw), ("dq", dq_raw)):
-            grouped = sb.tile([P, Q, PACK], BF16, name=name + "_grouped", align_bytes=64)
+        def quantize_rows(name, raw):
+            grouped = tile(name + "_grouped", [P, Q, PACK], BF16)
             nc.scalar.copy(
                 out=grouped[:].rearrange("p (c i) t -> p c t i", i=4),
                 in_=raw[:].rearrange("p t (c i) -> p c t i", i=4),
             )
-            codes = sb.tile([P, Q], U32, name=name + "_codes", align_bytes=64)
-            scales = sb.tile([P, Q], U8, name=name + "_scales", align_bytes=64)
+            codes = tile(name + "_codes", [P, Q], U32)
+            scales = tile(name + "_scales", [P, Q], U8)
             nc.vector.quantize_mx(out=codes[:].bitcast(FP8X4), scales=scales[:], in_=grouped[:].rearrange("p w j -> p (w j)"))
-            q_codes.append(codes)
-            q_scales.append(scales)
+            return codes, scales
 
-        pool = []
-        for j in range(blocks):
-            rows = sb.tile([P, T], F32, name="pool%d" % j, tag="pool%d" % j, align_bytes=64)
-            nc.sync.dma_start(out=rows[:], in_=vals[j * P : (j + 1) * P, :])
-            pool.append(rows)
+        keys = [gather_keys(0, None, None)]
+        rows = [quantize_rows("q", q_raw), quantize_rows("dq", dq_raw)]
+        keys.append(gather_keys(1, None, "q_grouped"))
 
-        a_ps = ps.tile([P, I], F32, name="a_ps", tag="a_ps")
-        ta_ps = ps.tile([P, I], F32, name="ta_ps")
-        for acc, codes, scales in ((a_ps, q_codes[0], q_scales[0]), (ta_ps, q_codes[1], q_scales[1])):
-            nc.tensor.matmul_mx(
-                out=acc[:], lhsT=codes[:].bitcast(FP8X4), lhsT_scale=scales[:],
-                rhs=k_codes[:].bitcast(FP4X4), rhs_scale=k_scales[:], start=True, stop=True,
+        a_ps = [bank("a%d" % half, [P, HALF]) for half in range(2)]
+        ta_ps = [bank("ta%d" % half, [P, HALF]) for half in range(2)]
+        for half in range(2):
+            for acc, (codes, scales) in zip((a_ps[half], ta_ps[half]), rows):
+                nc.tensor.matmul_mx(
+                    out=acc[:], lhsT=codes[:].bitcast(FP8X4), lhsT_scale=scales[:],
+                    rhs=keys[half][0][:].bitcast(FP4X4), rhs_scale=keys[half][1][:], start=True, stop=True,
+                )
+
+        soft = tile("soft", [P, I], BF16)
+        soft_sums = tile("soft_sums", [P, 3], F32)
+        sums = tile("sums", [P, 2 * G], F32)
+        for half in range(2):
+            nc.scalar.activation(
+                soft[:, half * HALF : (half + 1) * HALF], a_ps[half][:], ACT.Exp, scale=1.0 / SOFT,
+                accum_out=soft_sums[:, half : half + 1],
             )
-
-        soft = sb.tile([P, I], BF16, name="soft")
-        soft_sum = sb.tile([P, 1], F32, name="soft_sum")
-        nc.scalar.activation(soft[:], a_ps[:], ACT.Exp, scale=1.0 / SOFT, accum_out=soft_sum[:])
-        neg_shift = sb.tile([P, 1], F32, name="neg_shift")
+            for acc, first in ((a_ps[half], half * HALF_G), (ta_ps[half], G + half * HALF_G)):
+                nc.vector.tensor_reduce(sums[:, first : first + HALF_G], by_group(acc[:]), AX.X, ALU.add)
+        nc.scalar.activation(soft_sums[:, 2:3], soft_sums[:, 0:1], ACT.Identity, bias=soft_sums[:, 1:2])
+        neg_shift = tile("neg_shift", [P, 1], F32)
         nc.scalar.activation(
-            neg_shift[:], soft_sum[:].bitcast(U32), ACT.Copy, scale=-SOFT * math.log(2.0) / 2.0**23,
+            neg_shift[:], soft_sums[:, 2:3].bitcast(U32), ACT.Copy, scale=-SOFT * math.log(2.0) / 2.0**23,
             bias=SOFT * (127.0 * math.log(2.0) + math.log(I)),
         )
-        e = sb.tile([P, I], F32, name="e")
-        nc.scalar.activation(e[:], a_ps[:], ACT.Exp, bias=neg_shift[:])
+        e = tile("e", [P, I], F32)
+        for half in range(2):
+            nc.scalar.activation(e[:, half * HALF : (half + 1) * HALF], a_ps[half][:], ACT.Exp, bias=neg_shift[:])
 
-        sums = sb.tile([P, 2 * G], F32, name="sums", tag="pool0", align_bytes=64)
-        nc.vector.tensor_reduce(sums[:, 0:G], a_ps[:].rearrange("p (g r) -> p g r", r=GROUP), AX.X, ALU.add)
-        nc.vector.tensor_reduce(sums[:, G : 2 * G], ta_ps[:].rearrange("p (g r) -> p g r", r=GROUP), AX.X, ALU.add)
-        block_sums = sb.tile([P, 2 * B], F32, name="block_sums")
-        per_block = G // B
-        nc.vector.tensor_reduce(block_sums[:], sums[:].rearrange("p (b g) -> p b g", g=per_block), AX.X, ALU.add)
-        diff = sb.tile([P, 2 * G], F32, name="diff")
+        listed = [tile("listed%d" % j, [P, I], BF16) for j in range(4)]
+        nc.vector.tensor_copy(listed[0][:, 0:HALF], pool[0][:].indirect(half_lists[0]))
+        block_sums = listed[0][:, HALF : HALF + 4 * B].bitcast(F32)
+        nc.vector.tensor_reduce(block_sums, sums[:].rearrange("p (b g) -> p b g", g=PER_BLOCK), AX.X, ALU.add)
+        diff = tile("diff", [P, 2 * G], F32)
         nc.vector.scalar_tensor_tensor(
-            diff[:].rearrange("p (b g) -> p b g", g=per_block),
-            block_sums[:].unsqueeze(2).to_broadcast([P, 2 * B, per_block]), -1.0 / per_block,
-            sums[:].rearrange("p (b g) -> p b g", g=per_block), ALU.mult, ALU.add,
+            diff[:].rearrange("p (b g) -> p b g", g=PER_BLOCK),
+            block_sums.unsqueeze(2).to_broadcast([P, 2 * B, PER_BLOCK]), -1.0 / PER_BLOCK,
+            sums[:].rearrange("p (b g) -> p b g", g=PER_BLOCK), ALU.mult, ALU.add,
         )
-        th = sb.tile([P, G], F32, name="th")
+        th = tile("th", [P, G], F32)
         nc.scalar.activation(th[:], diff[:, 0:G], ACT.Tanh, scale=half_slope[:])
 
-        factor_ps = ps.tile([P, PACK, P], F32, name="factor_ps", tag="a_ps")
+        factor_ps = bank("factor_ps", [P, PACK, P], "a0")
         for t in range(PACK):
             nc.tensor.transpose(factor_ps[:, t, :], factor_cols[:, t : t + 1].to_broadcast([P, P]), ident[:])
 
-        def by_group(tile):
-            return tile[:].rearrange("p (g r) -> p g r", r=GROUP)
+        nc.vector.tensor_copy(listed[0][:, HALF:I], pool[0][:].indirect(half_lists[1]))
 
-        def spread(tile):
-            return tile[:].unsqueeze(2).to_broadcast([P, G, GROUP])
-
-        p = sb.tile([P, I], F32, name="p")
-        z = sb.tile([P, 1], F32, name="z")
-        nc.vector.scalar_tensor_tensor(by_group(p), spread(th), 1.0, by_group(e), ALU.add, ALU.mult, accum_out=z[:])
-        h = sb.tile([P, G], F32, name="h")
+        p = tile("p", [P, I], F32)
+        z = tile("z", [P, 1], F32)
+        nc.vector.scalar_tensor_tensor(by_group(p[:]), spread(th[:]), 1.0, by_group(e[:]), ALU.add, ALU.mult, accum_out=z[:])
+        h = tile("h", [P, G], F32)
         nc.vector.scalar_tensor_tensor(h[:], th[:], 1.0, diff[:, G : 2 * G], ALU.subtract, ALU.mult)
-        rz = sb.tile([P, 1], F32, name="rz")
+        rz = tile("rz", [P, 1], F32)
         nc.vector.reciprocal(rz[:], z[:])
-        u = sb.tile([P, I], F32, name="u")
-        nc.vector.scalar_tensor_tensor(by_group(u), spread(h), neg_half_slope[:], by_group(ta_ps), ALU.mult, ALU.add)
-        tp = sb.tile([P, I], F32, name="tp", tag="pool2", align_bytes=64)
-        c = sb.tile([P, 1], F32, name="c")
-        nc.vector.scalar_tensor_tensor(tp[:], u[:], rz[:], p[:], ALU.mult, ALU.mult, accum_out=c[:])
-        v = sb.tile([P, I], F32, name="v")
-        nc.vector.scalar_tensor_tensor(v[:], u[:], c[:], p[:], ALU.subtract, ALU.mult)
-        w = sb.tile([P, I], BF16, name="w")
-        nc.vector.scalar_tensor_tensor(
-            w[:].rearrange("p (n t) -> p n t", t=PACK), v[:].rearrange("p (n t) -> p n t", t=PACK), rz[:],
-            factor_ps[:].rearrange("p t n -> p n t"), ALU.mult, ALU.mult,
+        po = tile("po", [P, I], F32)
+        nc.vector.tensor_tensor(
+            po[:].rearrange("p (n t) -> p n t", t=PACK), factor_ps[:].rearrange("p t n -> p n t"),
+            p[:].rearrange("p (n t) -> p n t", t=PACK), ALU.mult,
         )
+        hs = tile("hs", [P, G], F32)
+        nc.vector.tensor_scalar(hs[:], h[:], neg_half_slope[:], rz[:], ALU.mult, ALU.mult)
+        u = tile("u", [P, I], F32)
+        for half in range(2):
+            nc.vector.scalar_tensor_tensor(
+                by_group(u[:, half * HALF : (half + 1) * HALF]), by_group(ta_ps[half][:]), rz[:],
+                spread(hs[:, half * HALF_G : (half + 1) * HALF_G]), ALU.mult, ALU.add,
+            )
+        nc.vector.tensor_copy(listed[2][:, 0:HALF], pool[2][:].indirect(half_lists[0]))
+        tp = tile("tp", [P, I], F32)
+        c = tile("c", [P, 1], F32)
+        nc.vector.scalar_tensor_tensor(tp[:], u[:], rz[:], p[:], ALU.mult, ALU.mult, accum_out=c[:])
+        nc.vector.tensor_copy(listed[2][:, HALF:I], pool[2][:].indirect(half_lists[1]))
+        w = tile("w", [P, I], BF16, "pool2")
+        nc.vector.scalar_tensor_tensor(w[:], u[:], c[:], po[:], ALU.subtract, ALU.mult)
+        nc.vector.tensor_copy(listed[3][:], pool[3][:].indirect(offsets[:]))
 
-        def turn_and_quantize(name, rows, bank, codes, grouped_tag):
-            words = rows[:].bitcast(F32)
+        rounded = tile("rounded", [P, T], BF16, "half_slope")
+        nc.scalar.activation(rounded[:], pool[1][:], ACT.Copy)
+        nc.scalar.activation(listed[1][:], rounded[:].indirect(offsets[:]), ACT.Copy)
+
+        def turn(source, turned, grouped):
+            words = source[:].bitcast(F32)
             for half in range(2):
-                nc.tensor.transpose(bank[:, half, :], words[:, half : I // 2 : 2], ident[:])
-            grouped = sb.tile([P, P * PACK], BF16, name=name + "_grouped", tag=grouped_tag, align_bytes=64)
+                nc.tensor.transpose(turned[:, half, :], words[:, half : I // 2 : 2], ident[:])
             nc.scalar.copy(
-                out=grouped[:].bitcast(F32).rearrange("p (x u) -> p x u", u=2), in_=bank[:].rearrange("p u x -> p x u")
+                out=grouped.bitcast(F32).rearrange("p (x u) -> p x u", u=2), in_=turned[:].rearrange("p u x -> p x u")
             )
-            scales = sb.tile([P, P], U8, name=name + "_scales", align_bytes=64)
-            nc.vector.quantize_mx(out=codes.bitcast(FP8X4), scales=scales[:], in_=grouped[:])
-            return scales
 
-        v_banks = [ps.tile([P, 2, P], F32, name="v_bank%d" % n) for n in range(2)]
-        listed = [sb.tile([P, I], BF16, name="listed%d" % j) for j in range(blocks)]
-        rounded = sb.tile([P, T], BF16, name="rounded", tag="rounded", align_bytes=64)
-        for j in range(blocks):
-            if j == 1:
-                for c0 in range(0, T, 512):
-                    nc.scalar.activation(rounded[:, c0 : c0 + 512], pool[j][:, c0 : c0 + 512], ACT.Copy)
-                nc.scalar.activation(listed[j][:], rounded[:].indirect(offsets[:]), ACT.Copy)
-            else:
-                nc.vector.tensor_copy(listed[j][:], pool[j][:].indirect(offsets[:]))
-        late_codes = sb.tile([P, 3, P], U32, name="late_codes", tag="pool3", align_bytes=64)
-        own_codes = sb.tile([P, 2, P], U32, name="own_codes", align_bytes=64)
-        w_bank = ps.tile([P, 2, P], F32, name="w_bank")
-        w_codes = late_codes[:, 0, :]
-        w_scales = turn_and_quantize("w", w, w_bank, w_codes, "rounded")
-        v_codes = [own_codes[:, 0, :], late_codes[:, 1, :], late_codes[:, 2, :], own_codes[:, 1, :]]
-        head_ps = ps.tile([P, (blocks - 1) * P], F32, name="head_ps")
-        tail_ps = ps.tile([P, P], F32, name="tail_ps")
-        for j in range(blocks):
-            scales = turn_and_quantize("v%d" % j, listed[j], v_banks[j % 2], v_codes[j], "v%d_grouped" % j)
-            acc = head_ps[:, j * P : (j + 1) * P] if j < blocks - 1 else tail_ps[:]
+        v_banks = [bank("v_bank%d" % n, [P, 2, P]) for n in range(2)]
+        pair_grouped = tile("pair_grouped", [P, 2 * I], BF16)
+        v2_grouped = tile("v2_grouped", [P, I], BF16, "half_slope")
+        w_grouped = tile("w_grouped", [P, I], BF16)
+        v3_grouped = tile("v3_grouped", [P, I], BF16)
+        turn(listed[0], v_banks[0], pair_grouped[:, 0:I])
+        turn(listed[1], v_banks[1], pair_grouped[:, I : 2 * I])
+        turn(listed[2], v_banks[0], v2_grouped[:])
+        turn(w, bank("w_bank", [P, 2, P], "a1"), w_grouped[:])
+        turn(listed[3], v_banks[1], v3_grouped[:])
+
+        late_codes = tile("late_codes", [P, 4 * P], U32, "pool3")
+        late_scales = tile("late_scales", [P, 4 * P], U8)
+        tail_codes = tile("tail_codes", [P, P], U32)
+        tail_scales = tile("tail_scales", [P, P], U8)
+        w_cols, pair_cols, v2_cols = slice(0, P), slice(P, 3 * P), slice(3 * P, 4 * P)
+        for grouped, cols in ((w_grouped, w_cols), (pair_grouped, pair_cols), (v2_grouped, v2_cols)):
+            nc.vector.quantize_mx(out=late_codes[:, cols].bitcast(FP8X4), scales=late_scales[:, cols], in_=grouped[:])
+        nc.vector.quantize_mx(out=tail_codes[:].bitcast(FP8X4), scales=tail_scales[:], in_=v3_grouped[:])
+
+        head_ps = bank("head_ps", [P, 3 * P])
+        tail_ps = bank("tail_ps", [P, P])
+        for acc, codes, scales in (
+            (head_ps[:, 0 : 2 * P], late_codes[:, pair_cols], late_scales[:, pair_cols]),
+            (head_ps[:, 2 * P : 3 * P], late_codes[:, v2_cols], late_scales[:, v2_cols]),
+            (tail_ps[:], tail_codes[:], tail_scales[:]),
+        ):
             nc.tensor.matmul_mx(
-                out=acc, lhsT=w_codes.bitcast(FP8X4), lhsT_scale=w_scales[:],
-                rhs=v_codes[j].bitcast(FP8X4), rhs_scale=scales[:], start=True, stop=True,
+                out=acc, lhsT=late_codes[:, w_cols].bitcast(FP8X4), lhsT_scale=late_scales[:, w_cols],
+                rhs=codes.bitcast(FP8X4), rhs_scale=scales, start=True, stop=True,
             )
-        head = sb.tile([P, (blocks - 1) * P], F32, name="head")
-        nc.scalar.copy(out=head[:], in_=head_ps[:])
-        nc.sync.dma_start(out=out[:, 0 : (blocks - 1) * P], in_=head[:])
-        tail = sb.tile([P, P], F32, name="tail")
+        head = tile("head", [P, 3 * P], F32)
+        nc.vector.tensor_copy(out=head[:], in_=head_ps[:])
+        nc.sync.dma_start(out=out[:, 0 : 3 * P], in_=head[:])
+        tail = tile("tail", [P, P], F32)
         nc.scalar.copy(out=tail[:], in_=tail_ps[:])
-        nc.sync.dma_start(out=out[:, (blocks - 1) * P : E], in_=tail[:])
+        nc.sync.dma_start(out=out[:, 3 * P : E], in_=tail[:])

@@ -108,11 +108,12 @@ def tile_attend_ttblockcontrast_kernel(tc, query, keys_words, keys_scales, steep
         keys.append(gather_keys(1, None, "q_grouped"))
 
         a_ps = [bank("a%d" % half, [P, HALF]) for half in range(2)]
-        ta_ps = [bank("ta%d" % half, [P, HALF]) for half in range(2)]
-        for half in range(2):
-            for acc, (codes, scales) in zip((a_ps[half], ta_ps[half]), rows):
+        ta_ps = bank("ta", [P, I])
+        ta_halves = [ta_ps[:, half * HALF : (half + 1) * HALF] for half in range(2)]
+        for accs, (codes, scales) in zip(([a_ps[0][:], a_ps[1][:]], ta_halves), rows):
+            for half in range(2):
                 nc.tensor.matmul_mx(
-                    out=acc[:], lhsT=codes[:].bitcast(FP8X4), lhsT_scale=scales[:],
+                    out=accs[half], lhsT=codes[:].bitcast(FP8X4), lhsT_scale=scales[:],
                     rhs=keys[half][0][:].bitcast(FP4X4), rhs_scale=keys[half][1][:], start=True, stop=True,
                 )
 
@@ -124,8 +125,10 @@ def tile_attend_ttblockcontrast_kernel(tc, query, keys_words, keys_scales, steep
                 soft[:, half * HALF : (half + 1) * HALF], a_ps[half][:], ACT.Exp, scale=1.0 / SOFT,
                 accum_out=soft_sums[:, half : half + 1],
             )
-            for acc, first in ((a_ps[half], half * HALF_G), (ta_ps[half], G + half * HALF_G)):
-                nc.vector.tensor_reduce(sums[:, first : first + HALF_G], by_group(acc[:]), AX.X, ALU.add)
+            nc.vector.tensor_reduce(
+                sums[:, half * HALF_G : (half + 1) * HALF_G], by_group(a_ps[half][:]), AX.X, ALU.add
+            )
+        nc.vector.tensor_reduce(sums[:, G : 2 * G], by_group(ta_ps[:]), AX.X, ALU.add)
         nc.scalar.activation(soft_sums[:, 2:3], soft_sums[:, 0:1], ACT.Identity, bias=soft_sums[:, 1:2])
         neg_shift = tile("neg_shift", [P, 1], F32)
         nc.scalar.activation(
@@ -149,10 +152,12 @@ def tile_attend_ttblockcontrast_kernel(tc, query, keys_words, keys_scales, steep
         th = tile("th", [P, G], F32)
         nc.scalar.activation(th[:], diff[:, 0:G], ACT.Tanh, scale=half_slope[:])
 
-        factor_ps = bank("factor_ps", [P, PACK, P], "a0")
+        factor_ps = bank("factor_ps", [P, PACK, P])
         for t in range(PACK):
             nc.tensor.transpose(factor_ps[:, t, :], factor_cols[:, t : t + 1].to_broadcast([P, P]), ident[:])
 
+        factor = tile("factor", [P, I], F32)
+        nc.scalar.copy(out=factor[:].rearrange("p (n t) -> p n t", t=PACK), in_=factor_ps[:].rearrange("p t n -> p n t"))
         nc.vector.tensor_copy(listed[0][:, HALF:I], pool[0][:].indirect(half_lists[1]))
 
         p = tile("p", [P, I], F32)
@@ -162,19 +167,12 @@ def tile_attend_ttblockcontrast_kernel(tc, query, keys_words, keys_scales, steep
         nc.vector.scalar_tensor_tensor(h[:], th[:], 1.0, diff[:, G : 2 * G], ALU.subtract, ALU.mult)
         rz = tile("rz", [P, 1], F32)
         nc.vector.reciprocal(rz[:], z[:])
-        po = tile("po", [P, I], F32)
-        nc.vector.tensor_tensor(
-            po[:].rearrange("p (n t) -> p n t", t=PACK), factor_ps[:].rearrange("p t n -> p n t"),
-            p[:].rearrange("p (n t) -> p n t", t=PACK), ALU.mult,
-        )
         hs = tile("hs", [P, G], F32)
         nc.vector.tensor_scalar(hs[:], h[:], neg_half_slope[:], rz[:], ALU.mult, ALU.mult)
+        po = tile("po", [P, I], F32, "h")
+        nc.gpsimd.tensor_tensor(po[:], p[:], factor[:], ALU.mult)
         u = tile("u", [P, I], F32)
-        for half in range(2):
-            nc.vector.scalar_tensor_tensor(
-                by_group(u[:, half * HALF : (half + 1) * HALF]), by_group(ta_ps[half][:]), rz[:],
-                spread(hs[:, half * HALF_G : (half + 1) * HALF_G]), ALU.mult, ALU.add,
-            )
+        nc.vector.scalar_tensor_tensor(by_group(u[:]), by_group(ta_ps[:]), rz[:], spread(hs[:]), ALU.mult, ALU.add)
         nc.vector.tensor_copy(listed[2][:, 0:HALF], pool[2][:].indirect(half_lists[0]))
         tp = tile("tp", [P, I], F32)
         c = tile("c", [P, 1], F32)

@@ -105,7 +105,7 @@ def tile_attend_ttblockcontrast_kernel(tc, query, keys_words, keys_scales, steep
 
         keys = [gather_keys(0, None, None)]
         rows = [quantize_rows("q", q_raw), quantize_rows("dq", dq_raw)]
-        keys.append(gather_keys(1, None, "q_grouped"))
+        keys.append(gather_keys(1, None, "q_raw"))
 
         a_ps = [bank("a%d" % half, [P, HALF]) for half in range(2)]
         ta_ps = bank("ta", [P, I])
@@ -149,35 +149,36 @@ def tile_attend_ttblockcontrast_kernel(tc, query, keys_words, keys_scales, steep
             block_sums.unsqueeze(2).to_broadcast([P, 2 * B, PER_BLOCK]), -1.0 / PER_BLOCK,
             sums[:].rearrange("p (b g) -> p b g", g=PER_BLOCK), ALU.mult, ALU.add,
         )
+        dn = tile("dn", [P, G], F32)
+        nc.scalar.activation(dn[:], diff[:, G : 2 * G], ACT.Copy, scale=neg_half_slope[:])
         th = tile("th", [P, G], F32)
         nc.scalar.activation(th[:], diff[:, 0:G], ACT.Tanh, scale=half_slope[:])
 
-        factor_ps = bank("factor_ps", [P, PACK, P])
+        factor_ps = bank("factor_ps", [P, PACK, P], "a0")
         for t in range(PACK):
             nc.tensor.transpose(factor_ps[:, t, :], factor_cols[:, t : t + 1].to_broadcast([P, P]), ident[:])
 
-        factor = tile("factor", [P, I], F32)
-        nc.scalar.copy(out=factor[:].rearrange("p (n t) -> p n t", t=PACK), in_=factor_ps[:].rearrange("p t n -> p n t"))
         nc.vector.tensor_copy(listed[0][:, HALF:I], pool[0][:].indirect(half_lists[1]))
 
+        h = tile("h", [P, G], F32)
+        nc.vector.scalar_tensor_tensor(h[:], th[:], 1.0, dn[:], ALU.subtract, ALU.mult)
         p = tile("p", [P, I], F32)
         z = tile("z", [P, 1], F32)
         nc.vector.scalar_tensor_tensor(by_group(p[:]), spread(th[:]), 1.0, by_group(e[:]), ALU.add, ALU.mult, accum_out=z[:])
-        h = tile("h", [P, G], F32)
-        nc.vector.scalar_tensor_tensor(h[:], th[:], 1.0, diff[:, G : 2 * G], ALU.subtract, ALU.mult)
+        u = tile("u", [P, I], F32)
+        nc.vector.tensor_tensor(by_group(u[:]), by_group(ta_ps[:]), spread(h[:]), ALU.add)
         rz = tile("rz", [P, 1], F32)
         nc.vector.reciprocal(rz[:], z[:])
-        hs = tile("hs", [P, G], F32)
-        nc.vector.tensor_scalar(hs[:], h[:], neg_half_slope[:], rz[:], ALU.mult, ALU.mult)
-        po = tile("po", [P, I], F32, "h")
-        nc.gpsimd.tensor_tensor(po[:], p[:], factor[:], ALU.mult)
-        u = tile("u", [P, I], F32)
-        nc.vector.scalar_tensor_tensor(by_group(u[:]), by_group(ta_ps[:]), rz[:], spread(hs[:]), ALU.mult, ALU.add)
         nc.vector.tensor_copy(listed[2][:, 0:HALF], pool[2][:].indirect(half_lists[0]))
         tp = tile("tp", [P, I], F32)
         c = tile("c", [P, 1], F32)
         nc.vector.scalar_tensor_tensor(tp[:], u[:], rz[:], p[:], ALU.mult, ALU.mult, accum_out=c[:])
         nc.vector.tensor_copy(listed[2][:, HALF:I], pool[2][:].indirect(half_lists[1]))
+        po = tile("po", [P, I], F32)
+        nc.vector.scalar_tensor_tensor(
+            po[:].rearrange("p (n t) -> p n t", t=PACK), p[:].rearrange("p (n t) -> p n t", t=PACK), rz[:],
+            factor_ps[:].rearrange("p t n -> p n t"), ALU.mult, ALU.mult,
+        )
         w = tile("w", [P, I], BF16, "pool2")
         nc.vector.scalar_tensor_tensor(w[:], u[:], c[:], po[:], ALU.subtract, ALU.mult)
         nc.vector.tensor_copy(listed[3][:], pool[3][:].indirect(offsets[:]))
@@ -195,14 +196,15 @@ def tile_attend_ttblockcontrast_kernel(tc, query, keys_words, keys_scales, steep
             )
 
         v_banks = [bank("v_bank%d" % n, [P, 2, P]) for n in range(2)]
-        pair_grouped = tile("pair_grouped", [P, 2 * I], BF16)
-        v2_grouped = tile("v2_grouped", [P, I], BF16, "half_slope")
-        w_grouped = tile("w_grouped", [P, I], BF16)
+        pair_grouped = tile("pair_grouped", [P, 2 * I], BF16, "pool1")
+        late_grouped = tile("late_grouped", [P, 2 * I], BF16, "half_slope")
+        v2_grouped = late_grouped[:, 0:I]
+        w_grouped = late_grouped[:, I : 2 * I]
         v3_grouped = tile("v3_grouped", [P, I], BF16)
         turn(listed[0], v_banks[0], pair_grouped[:, 0:I])
         turn(listed[1], v_banks[1], pair_grouped[:, I : 2 * I])
-        turn(listed[2], v_banks[0], v2_grouped[:])
-        turn(w, bank("w_bank", [P, 2, P], "a1"), w_grouped[:])
+        turn(listed[2], v_banks[0], v2_grouped)
+        turn(w, bank("w_bank", [P, 2, P], "a1"), w_grouped)
         turn(listed[3], v_banks[1], v3_grouped[:])
 
         late_codes = tile("late_codes", [P, 4 * P], U32, "pool3")
@@ -210,8 +212,8 @@ def tile_attend_ttblockcontrast_kernel(tc, query, keys_words, keys_scales, steep
         tail_codes = tile("tail_codes", [P, P], U32)
         tail_scales = tile("tail_scales", [P, P], U8)
         w_cols, pair_cols, v2_cols = slice(0, P), slice(P, 3 * P), slice(3 * P, 4 * P)
-        for grouped, cols in ((w_grouped, w_cols), (pair_grouped, pair_cols), (v2_grouped, v2_cols)):
-            nc.vector.quantize_mx(out=late_codes[:, cols].bitcast(FP8X4), scales=late_scales[:, cols], in_=grouped[:])
+        for grouped, cols in ((w_grouped, w_cols), (pair_grouped[:], pair_cols), (v2_grouped, v2_cols)):
+            nc.vector.quantize_mx(out=late_codes[:, cols].bitcast(FP8X4), scales=late_scales[:, cols], in_=grouped)
         nc.vector.quantize_mx(out=tail_codes[:].bitcast(FP8X4), scales=tail_scales[:], in_=v3_grouped[:])
 
         head_ps = bank("head_ps", [P, 3 * P])

import math
from contextlib import ExitStack

import concourse.mybir as mybir
from concourse.masks import make_identity

D, E, T, I, Q, G, B = 512, 512, 2048, 512, 128, 64, 8
FLOPS = 2 * 2 * D * Q * I + 2 * I * Q * E

F32 = mybir.dt.float32
BF16 = mybir.dt.bfloat16
I32 = mybir.dt.int32
U32 = mybir.dt.uint32
U16 = mybir.dt.uint16
U8 = mybir.dt.uint8
FP8X4 = mybir.dt.float8_e4m3fn_x4
FP4X4 = mybir.dt.float4_e2m1fn_x4
ALU = mybir.AluOpType
ACT = mybir.ActivationFunctionType
AX = mybir.AxisListType

P = 128
PACK = 4
GROUP = I // G
PER_BLOCK = G // B
HALF = I // 2
HALF_G = G // 2
SOFT = 8.0
CHUNK = 512


def tile_attend_ttblockcontrast_kernel(tc, query, keys_words, keys_scales, steep, dquery, slot_factor, vals, offs, out):
    nc = tc.nc
    with ExitStack() as ctx:
        sb = ctx.enter_context(tc.tile_pool(name="sb", bufs=1))
        ps = ctx.enter_context(tc.psum_pool(name="ps", bufs=1))

        def tile(name, shape, dtype, tag=None):
            return sb.tile(shape, dtype, name=name, tag=tag or name, align_bytes=64)

        def bank(name, shape, tag=None):
            return ps.tile(shape, F32, name=name, tag=tag or name)

        def by_group(ap):
            return ap.rearrange("p (g r) -> p g r", r=GROUP)

        def spread(ap):
            return ap.unsqueeze(2).to_broadcast([P, ap.shape[1], GROUP])

        offsets = sb.tile([P, I // 16], U16, name="offsets")
        nc.sync.dma_start(offsets[:], offs)
        half_lists = [offsets[:, 0 : HALF // 16], offsets[:, HALF // 16 : I // 16]]

        key_words = tile("key_words", [P, T], U16)
        nc.sync.dma_start(out=key_words[:].bitcast(I32), in_=keys_words[0].bitcast(I32))
        key_bytes = tile("key_bytes", [P, T], U8)
        nc.gpsimd.memset(key_bytes[:].bitcast(I32), 0)
        for quad in range(4):
            nc.sync.dma_start(
                out=key_bytes[32 * quad : 32 * quad + 4, :].bitcast(I32),
                in_=keys_scales[0, 4 * quad : 4 * quad + 4, :].bitcast(I32),
            )
        q_raw = tile("q_raw", [P, PACK, Q], F32)
        nc.sync.dma_start(out=q_raw[:], in_=query.rearrange("(p j) w -> p j w", j=PACK))
        dq_raw = tile("dq_raw", [P, PACK, Q], F32)
        nc.sync.dma_start(out=dq_raw[:], in_=dquery.rearrange("(p j) w -> p j w", j=PACK))
        pool = [tile("pool%d" % j, [P, T], F32) for j in range(4)]
        nc.sync.dma_start(out=pool[0][:], in_=vals[0:P, :])
        steep_col = tile("steep_col", [P, 1], F32)
        nc.sync.dma_start(out=steep_col[:], in_=steep)
        factor_cols = tile("factor_cols", [P, PACK], F32)
        nc.sync.dma_start(out=factor_cols[:], in_=slot_factor.rearrange("o (p t) -> p (o t)", t=PACK))
        for j in range(1, 4):
            nc.sync.dma_start(out=pool[j][:], in_=vals[j * P : (j + 1) * P, :])

        warm_in = tile("warm_in", [P, 1], F32)
        warm_out = tile("warm_out", [P, 1], F32)
        nc.vector.memset(warm_in[:], 0.0)
        nc.scalar.activation(warm_out[:], warm_in[:], ACT.Exp)

        ident = tile("ident", [P, P], F32)
        make_identity(nc, ident[:])
        half_slope = tile("half_slope", [P, 1], F32)
        nc.gpsimd.tensor_scalar(half_slope[:], steep_col[:], 0.5 / GROUP, 0.0, ALU.mult, ALU.add)
        neg_half_slope = tile("neg_half_slope", [P, 1], F32)
        nc.gpsimd.tensor_scalar(neg_half_slope[:], steep_col[:], -0.5 / GROUP, 0.0, ALU.mult, ALU.add)

        def gather_keys(half, codes_tag, scales_tag):
            codes = tile("k_codes%d" % half, [P, HALF], U16, codes_tag)
            nc.vector.tensor_copy(codes[:], key_words[:].indirect(half_lists[half]))
            scales = tile("k_scales%d" % half, [P, HALF], U8, scales_tag)
            nc.vector.tensor_copy(scales[:], key_bytes[:].indirect(half_lists[half]))
            return codes, scales

        def quantize_rows(name, raw):
            grouped = tile(name + "_grouped", [P, Q, PACK], BF16)
            nc.scalar.copy(
                out=grouped[:].rearrange("p (c i) t -> p c t i", i=4),
                in_=raw[:].rearrange("p t (c i) -> p c t i", i=4),
            )
            codes = tile(name + "_codes", [P, Q], U32)
            scales = tile(name + "_scales", [P, Q], U8)
            nc.vector.quantize_mx(out=codes[:].bitcast(FP8X4), scales=scales[:], in_=grouped[:].rearrange("p w j -> p (w j)"))
            return codes, scales

        keys = [gather_keys(0, None, None)]
        rows = [quantize_rows("q", q_raw), quantize_rows("dq", dq_raw)]
        keys.append(gather_keys(1, None, "q_raw"))

        a_ps = [bank("a%d" % half, [P, HALF]) for half in range(2)]
        ta_ps = bank("ta", [P, I])
        ta_halves = [ta_ps[:, half * HALF : (half + 1) * HALF] for half in range(2)]
        for accs, (codes, scales) in zip(([a_ps[0][:], a_ps[1][:]], ta_halves), rows):
            for half in range(2):
                nc.tensor.matmul_mx(
                    out=accs[half], lhsT=codes[:].bitcast(FP8X4), lhsT_scale=scales[:],
                    rhs=keys[half][0][:].bitcast(FP4X4), rhs_scale=keys[half][1][:], start=True, stop=True,
                )

        soft = tile("soft", [P, I], BF16)
        soft_sums = tile("soft_sums", [P, 3], F32)
        sums = tile("sums", [P, 2 * G], F32)
        for half in range(2):
            nc.scalar.activation(
                soft[:, half * HALF : (half + 1) * HALF], a_ps[half][:], ACT.Exp, scale=1.0 / SOFT,
                accum_out=soft_sums[:, half : half + 1],
            )
            nc.vector.tensor_reduce(
                sums[:, half * HALF_G : (half + 1) * HALF_G], by_group(a_ps[half][:]), AX.X, ALU.add
            )
        nc.vector.tensor_reduce(sums[:, G : 2 * G], by_group(ta_ps[:]), AX.X, ALU.add)
        nc.scalar.activation(soft_sums[:, 2:3], soft_sums[:, 0:1], ACT.Identity, bias=soft_sums[:, 1:2])
        neg_shift = tile("neg_shift", [P, 1], F32)
        nc.scalar.activation(
            neg_shift[:], soft_sums[:, 2:3].bitcast(U32), ACT.Copy, scale=-SOFT * math.log(2.0) / 2.0**23,
            bias=SOFT * (127.0 * math.log(2.0) + math.log(I)),
        )
        e = tile("e", [P, I], F32)
        for half in range(2):
            nc.scalar.activation(e[:, half * HALF : (half + 1) * HALF], a_ps[half][:], ACT.Exp, bias=neg_shift[:])

        listed = [tile("listed%d" % j, [P, I], BF16) for j in range(4)]
        nc.vector.tensor_copy(listed[0][:, 0:HALF], pool[0][:].indirect(half_lists[0]))
        block_sums = listed[0][:, HALF : HALF + 4 * B].bitcast(F32)
        nc.vector.tensor_reduce(block_sums, sums[:].rearrange("p (b g) -> p b g", g=PER_BLOCK), AX.X, ALU.add)
        diff = tile("diff", [P, 2 * G], F32)
        nc.vector.scalar_tensor_tensor(
            diff[:].rearrange("p (b g) -> p b g", g=PER_BLOCK),
            block_sums.unsqueeze(2).to_broadcast([P, 2 * B, PER_BLOCK]), -1.0 / PER_BLOCK,
            sums[:].rearrange("p (b g) -> p b g", g=PER_BLOCK), ALU.mult, ALU.add,
        )
        dn = tile("dn", [P, G], F32)
        nc.scalar.activation(dn[:], diff[:, G : 2 * G], ACT.Copy, scale=neg_half_slope[:])
        th = tile("th", [P, G], F32)
        nc.scalar.activation(th[:], diff[:, 0:G], ACT.Tanh, scale=half_slope[:])

        factor_ps = bank("factor_ps", [P, PACK, P], "a0")
        for t in range(PACK):
            nc.tensor.transpose(factor_ps[:, t, :], factor_cols[:, t : t + 1].to_broadcast([P, P]), ident[:])

        nc.vector.tensor_copy(listed[0][:, HALF:I], pool[0][:].indirect(half_lists[1]))

        h = tile("h", [P, G], F32)
        nc.vector.scalar_tensor_tensor(h[:], th[:], 1.0, dn[:], ALU.subtract, ALU.mult)
        p = tile("p", [P, I], F32)
        z = tile("z", [P, 1], F32)
        nc.vector.scalar_tensor_tensor(by_group(p[:]), spread(th[:]), 1.0, by_group(e[:]), ALU.add, ALU.mult, accum_out=z[:])
        u = tile("u", [P, I], F32)
        nc.vector.tensor_tensor(by_group(u[:]), by_group(ta_ps[:]), spread(h[:]), ALU.add)
        rz = tile("rz", [P, 1], F32)
        nc.vector.reciprocal(rz[:], z[:])
        nc.vector.tensor_copy(listed[2][:, 0:HALF], pool[2][:].indirect(half_lists[0]))
        tp = tile("tp", [P, I], F32)
        c = tile("c", [P, 1], F32)
        nc.vector.scalar_tensor_tensor(tp[:], u[:], rz[:], p[:], ALU.mult, ALU.mult, accum_out=c[:])
        nc.vector.tensor_copy(listed[2][:, HALF:I], pool[2][:].indirect(half_lists[1]))
        po = tile("po", [P, I], F32)
        nc.vector.scalar_tensor_tensor(
            po[:].rearrange("p (n t) -> p n t", t=PACK), p[:].rearrange("p (n t) -> p n t", t=PACK), rz[:],
            factor_ps[:].rearrange("p t n -> p n t"), ALU.mult, ALU.mult,
        )
        w = tile("w", [P, I], BF16, "pool2")
        nc.vector.scalar_tensor_tensor(w[:], u[:], c[:], po[:], ALU.subtract, ALU.mult)
        nc.vector.tensor_copy(listed[3][:], pool[3][:].indirect(offsets[:]))

        rounded = tile("rounded", [P, T], BF16, "half_slope")
        nc.scalar.activation(rounded[:], pool[1][:], ACT.Copy)
        nc.scalar.activation(listed[1][:], rounded[:].indirect(offsets[:]), ACT.Copy)

        def turn(source, turned, grouped):
            words = source[:].bitcast(F32)
            for half in range(2):
                nc.tensor.transpose(turned[:, half, :], words[:, half : I // 2 : 2], ident[:])
            nc.scalar.copy(
                out=grouped.bitcast(F32).rearrange("p (x u) -> p x u", u=2), in_=turned[:].rearrange("p u x -> p x u")
            )

        v_banks = [bank("v_bank%d" % n, [P, 2, P]) for n in range(2)]
        pair_grouped = tile("pair_grouped", [P, 2 * I], BF16, "pool1")
        late_grouped = tile("late_grouped", [P, 2 * I], BF16, "half_slope")
        v2_grouped = late_grouped[:, 0:I]
        w_grouped = late_grouped[:, I : 2 * I]
        v3_grouped = tile("v3_grouped", [P, I], BF16)
        turn(listed[0], v_banks[0], pair_grouped[:, 0:I])
        turn(listed[1], v_banks[1], pair_grouped[:, I : 2 * I])
        turn(listed[2], v_banks[0], v2_grouped)
        turn(w, bank("w_bank", [P, 2, P], "a1"), w_grouped)
        turn(listed[3], v_banks[1], v3_grouped[:])

        late_codes = tile("late_codes", [P, 4 * P], U32, "pool3")
        late_scales = tile("late_scales", [P, 4 * P], U8)
        tail_codes = tile("tail_codes", [P, P], U32)
        tail_scales = tile("tail_scales", [P, P], U8)
        w_cols, pair_cols, v2_cols = slice(0, P), slice(P, 3 * P), slice(3 * P, 4 * P)
        for grouped, cols in ((w_grouped, w_cols), (pair_grouped[:], pair_cols), (v2_grouped, v2_cols)):
            nc.vector.quantize_mx(out=late_codes[:, cols].bitcast(FP8X4), scales=late_scales[:, cols], in_=grouped)
        nc.vector.quantize_mx(out=tail_codes[:].bitcast(FP8X4), scales=tail_scales[:], in_=v3_grouped[:])

        head_ps = bank("head_ps", [P, 3 * P])
        tail_ps = bank("tail_ps", [P, P])
        for acc, codes, scales in (
            (head_ps[:, 0 : 2 * P], late_codes[:, pair_cols], late_scales[:, pair_cols]),
            (head_ps[:, 2 * P : 3 * P], late_codes[:, v2_cols], late_scales[:, v2_cols]),
            (tail_ps[:], tail_codes[:], tail_scales[:]),
        ):
            nc.tensor.matmul_mx(
                out=acc, lhsT=late_codes[:, w_cols].bitcast(FP8X4), lhsT_scale=late_scales[:, w_cols],
                rhs=codes.bitcast(FP8X4), rhs_scale=scales, start=True, stop=True,
            )
        head = tile("head", [P, 3 * P], F32)
        nc.vector.tensor_copy(out=head[:], in_=head_ps[:])
        nc.sync.dma_start(out=out[:, 0 : 3 * P], in_=head[:])
        tail = tile("tail", [P, P], F32)
        nc.scalar.copy(out=tail[:], in_=tail_ps[:])
        nc.sync.dma_start(out=out[:, 3 * P : E], in_=tail[:])
